import numpy as np, ml_dtypes
CORES = [113,118,241,246]
N = 4
BF = ml_dtypes.bfloat16
def gentries(a):
    return np.ascontiguousarray(a.reshape(8, 16, -1).transpose(0, 2, 1)).reshape(8, -1)
def gtable(e):
    e = np.asarray(e); return np.ascontiguousarray(e.reshape(8, -1, 16).transpose(0, 2, 1)).reshape(128, -1).astype(np.int32)
S, n, M, CAP, DM = 2, 1792, 16, 320, 63
def lists(prev, ship, heads):
    a = [np.stack([gentries(x) for x in v]).astype(np.int64) for v in (prev, ship, heads)]
    return a[0].reshape(N, 8, S - 1, n), a[1].reshape(N, 8, S - 1, N, CAP), a[2].reshape(N, 8, S, M)
def before(pv, sh):
    r = np.arange(N).reshape(-1, 1, 1, 1); g = np.arange(8).reshape(1, -1, 1, 1); t = np.arange(S - 1).reshape(1, 1, -1, 1)
    x = np.maximum(pv - n, 0); q = x // CAP; e = sh[q, g, t, r, x % CAP]
    return np.where(pv < n, r * n + pv, np.where(e < 0, -1, q * n + e))
def counts(rng, w, swaps):
    A = np.zeros((N, N), np.int64); i = np.arange(N)
    for k in range(1, N): A[i, (i + k) % N] = w[k - 1]
    A[i, i] = n - np.add.reduce(A, axis=1)
    lim = np.where(np.eye(N, dtype=bool), n, CAP)
    for k in range(swaps):
        a, b = rng.permutation(N)[:2]; c, e = rng.permutation(N)[:2]
        m = int(min(A[a, e], A[b, c], lim[a, c] - A[a, c], lim[b, e] - A[b, e])); x = int(rng.integers(0, m // 3 + 1))
        A[a, c] += x; A[b, e] += x; A[a, e] -= x; A[b, c] -= x
    return A
def mixed(rng):
    return [[counts(rng, rng.integers(CAP // 4, 3 * CAP // 4, N - 1), 3 * N) for g in range(8)] for t in range(S - 1)]
def evens(rng):
    h = np.arange(M) * (n // M) + rng.integers(-(n // M // 3), n // M // 3 + 1, (N, 8, S, M)); h[..., 0] = 0
    return h
def uneven(rng):
    m = np.arange(M); b = rng.integers(0, M, (N, 8, S, 1))
    return np.where(m <= b, m, n - M + m)
def shop(rng, hd, ways, noise, turn=False):
    pv = np.zeros((N, 8, S - 1, n), np.int64); sh = np.full((N, 8, S - 1, N, CAP), -1, np.int64); ph = np.zeros((N, 8, S, n), np.int64); i = np.arange(n)
    for r in range(N):
        for g in range(8):
            for t in range(S):
                h = hd[r, g, t]; m = np.searchsorted(h, i, side="right") - 1; size = np.append(h, n)[1:] - h
                ph[r, g, t] = (2 * (i - h[m]) + 1) * 32768 // size[m]
    for t in range(S - 1):
        for g in range(8):
            A = ways[t][g]; num = [[] for r in range(N)]; key = [[] for r in range(N)]
            for q in range(N):
                o = rng.permutation(n); e = np.add.accumulate(A[q])
                for r in range(N):
                    u = o[e[r] - A[q, r]:e[r]]
                    if r == q: num[r].append(u)
                    else:
                        sh[q, g, t, r, :len(u)] = u; num[r].append(n + CAP * q + np.arange(len(u)))
                    key[r].append(ph[q, g, t, u])
            for r in range(N):
                a = np.concatenate(num[r]); k = np.concatenate(key[r]) + rng.integers(-noise, noise + 1, n)
                if turn: k = 65536 - k
                place = np.argsort(ph[r, g, t + 1] * n + rng.permutation(n))
                pv[r, g, t, place] = a[np.argsort(k)]
    return {"prev": np.stack([gtable(x.reshape(8, -1)) for x in pv]), "ship": np.stack([gtable(x.reshape(8, -1)) for x in sh]), "heads": np.stack([gtable(x.reshape(8, -1)) for x in hd])}
def times_of(rng):
    top = rng.integers(15, DM + 1, (N, 128, 1))
    return np.floor(rng.random((N, 128, S * n)) * (top + 1)).astype(BF)
def setup_inputs(rng):
    return {"dur": times_of(rng), **shop(rng, evens(rng), mixed(rng), 1500)}
def setup_inputs_full(rng):
    ways = [[counts(rng, [[CAP] * (N - 1), [0] * (N - 1), [CAP] + [0] * (N - 2), [1] * (N - 1)][(g + t) % 4], 0) for g in range(8)] for t in range(S - 1)]
    return {"dur": times_of(rng), **shop(rng, evens(rng), ways, 1500)}
def setup_inputs_machines(rng):
    hd = uneven(rng)
    return {"dur": rng.integers(DM - 15, DM + 1, (N, 128, S * n)).astype(np.float32).astype(BF), **shop(rng, hd, mixed(rng), 1 << 20)}
def setup_inputs_turned(rng):
    ways = mixed(rng)
    for t in range(S - 1):
        for g in range(0, 8, 2): ways[t][g] = counts(rng, [0] * (N - 1), 0)
    return {"dur": np.full((N, 128, S * n), DM, np.float32).astype(BF), **shop(rng, uneven(rng), ways, 0, turn=True)}
def setup_inputs_ties(rng):
    c = rng.integers(1, DM + 1, (N, 128, 1)); z = rng.integers(0, 4, (N, 128, S * n)) > 0; z[:, ::2] = True
    c[:, ::2] = 8
    return {"dur": np.where(z, c, 0).astype(np.float32).astype(BF), **shop(rng, evens(rng), mixed(rng), 1500)}
def setup_inputs_spread(rng):
    e = rng.integers(0, 7, (N, 1, S * n))
    return {"dur": np.floor(rng.random((N, 128, S * n)) * np.exp2(e)).astype(BF), **shop(rng, evens(rng), mixed(rng), 6000)}
def check_inputs(d):
    bad = []; v = d["dur"].astype(np.float32)
    if not (np.isfinite(v).all() and (v >= 0).all() and (v <= DM).all() and (v == np.floor(v)).all()): bad.append("durations")
    pv, sh, hd = lists(d["prev"], d["ship"], d["heads"])
    if (hd[..., 0] != 0).any() or (hd[..., 1:] <= hd[..., :-1]).any() or (hd[..., -1] >= n).any(): bad.append("heads")
    own = np.arange(N)
    if (sh < -1).any() or (sh >= n).any() or ((sh[..., 1:] >= 0) & (sh[..., :-1] < 0)).any() or (sh[own, :, :, own] != -1).any(): bad.append("ship")
    if (pv < 0).any() or (pv >= n + N * CAP).any(): bad.append("prev")
    if bad: return bad
    b = np.sort(before(pv, sh).transpose(1, 2, 0, 3).reshape(8, S - 1, N * n), axis=-1)
    if (b != np.arange(N * n)).any() or np.count_nonzero(sh >= 0) != np.count_nonzero(pv >= n): bad.append("jobs")
    return bad
def reference(dur, prev, ship, heads):
    pv, sh, hd = lists(prev, ship, heads); g = np.arange(8)
    b = before(pv, sh).transpose(2, 3, 0, 1)
    d = np.ascontiguousarray(dur.astype(np.float32).astype(np.int64).reshape(N, 8, 16, S, n).transpose(3, 4, 0, 1, 2))
    st = np.zeros((N, 8, S, n), bool); np.put_along_axis(st, hd, True, axis=-1)
    st = np.ascontiguousarray(st.transpose(2, 3, 0, 1))[..., None]
    C = np.zeros((S, n, N, 8, 16), np.int64)
    for t in range(S):
        R = np.zeros((n, N, 8, 16), np.int64) if t == 0 else C[t - 1].transpose(1, 0, 2, 3).reshape(N * n, 8, 16)[b[t - 1], g]
        m = np.zeros((N, 8, 16), np.int64)
        for i in range(n):
            m = np.maximum(np.where(st[t, i], 0, m), R[i]) + d[t, i]; C[t, i] = m
    D = np.max(C[S - 1], axis=(0, 1))
    sl = np.zeros((S - 1, n, N, 8, 16), np.int64); B = np.zeros((n, N, 8, 16), np.int64)
    for t in range(S - 1, -1, -1):
        if t == S - 1: Q = np.broadcast_to(D, (n, N, 8, 16))
        else:
            w = np.zeros((N * n, 8, 16), np.int64); w[b[t], g] = B; Q = w.reshape(N, n, 8, 16).transpose(1, 0, 2, 3)
        B = np.zeros((n, N, 8, 16), np.int64); m = np.broadcast_to(D, (N, 8, 16))
        for i in range(n - 1, -1, -1):
            F = np.minimum(m, Q[i])
            if t < S - 1: sl[t, i] = F - C[t, i]
            B[i] = F - d[t, i]; m = np.where(st[t, i], D, B[i])
    y = sl.transpose(2, 3, 4, 0, 1).reshape(N, 128, (S - 1) * n)
    return {"y": y.astype(np.float32)}

@@ -1,0 +1,226 @@
+from concourse.bass import DstId, RemoteDMATransfer
+from concourse.mybir import AluOpType, AxisListType, ActivationFunctionType
+
+n, CAP, NR = 1792, 320, 4
+WW = n + NR * CAP
+LW = 2240
+OFF_T, OFF_C, BIG = 32.0, 8388608.0, 12582912.0
+T_CHUNKS = [(1536, 1792), (896, 1536), (0, 896)]
+BANKS = [(0, 512), (512, 1024), (1024, 1536), (1536, 1792)]
+FILL = 384
+Y_V1, Y_S = 448, 1120
+
+SCRATCH = {
+    "d1": ("sbuf", [128, n], "bfloat16"),
+    "d0": ("sbuf", [128, n], "bfloat16"),
+    "A": ("sbuf", [128, n + 16], "bfloat16"),
+    "K": ("sbuf", [128, 48], "bfloat16"),
+    "hd": ("sbuf", [128, 2], "int32"),
+    "pv": ("sbuf", [128, 112], "int32"),
+    "sh": ("sbuf", [128, 80], "int32"),
+    "hoff": ("sbuf", [128, 4], "uint16"),
+    "poff": ("sbuf", [128, 112], "uint16"),
+    "goff": ("sbuf", [128, 80], "uint16"),
+    "soff": ("sbuf", [128, 80], "uint16"),
+    "dump": ("sbuf", [128, 80], "int32"),
+    "s1": ("sbuf", [128, 80], "int32"),
+    "s2": ("sbuf", [128, 80], "int32"),
+    "T1": ("sbuf", [128, n], "float32"),
+    "W": ("sbuf", [128, WW], "float32"),
+    "C0": ("sbuf", [128, n], "float32"),
+    "Cp": ("psum", [128, 2048], "float32"),
+    "a": ("sbuf", [128, 968], "float32"),
+    "dl": ("sbuf", [128, 968], "float32"),
+    "land": ("sbuf", [128, 968], "float32"),
+    "run": ("sbuf", [128, 968], "float32"),
+    "L": ("sbuf", [128, LW], "float32"),
+    "Dl": ("sbuf", [128, 4], "float32"),
+    "Dland": ("sbuf", [128, 4], "float32"),
+    "Dt": ("sbuf", [128, 4], "float32"),
+    "M": ("sbuf", [128, n], "float32"),
+    "Y": ("sbuf", [128, n], "float32"),
+}
+NEV = 100
+SEMAPHORES = ["e%d" % k for k in range(NEV)] + ["arr0", "arr1", "arr2", "arrD", "sent"]
+
+
+def bits(engines):
+    m = 0
+    for e in engines:
+        m |= 1 << e
+    return m
+
+
+def rev(a, b):
+    return slice(b - 1, a - 1 if a > 0 else None, -1)
+
+
+def rank_program(g, core, T, topo):
+    rank = T.rank_of(core)
+    if rank is None:
+        return
+    ALU, ACT = AluOpType, ActivationFunctionType
+    V, S, Q = g.vector, g.scalar, g.sync
+    queues = {"G": g, "V": V, "S": S, "Q": Q}
+
+    others = [c for c in T.cores if c != core]
+    near = [c for c in others if c in topo.cores_of(core)]
+    far = [c for c in others if c not in near]
+    far = [c for c in far if topo.die(c) == topo.die(core)] + [c for c in far if topo.die(c) != topo.die(core)]
+    peers = [far[0], near[0], far[1]]
+    pr = [T.rank_of(c) for c in peers]
+    far_eng = topo.engines(core, far[0])
+    near_eng = [e for e in topo.engines(core, near[0]) if e not in far_eng]
+    half = len(far_eng) // 2
+
+    count = [0]
+    seen = {q: set() for q in queues}
+    events = {}
+
+    def wait(q, *evs):
+        for ev in evs:
+            if ev not in seen[q]:
+                seen[q].add(ev)
+                queues[q].wait_ge(T.sem[ev], events[ev])
+
+    def mark(ins, val=1):
+        ev = "e%d" % count[0]
+        count[0] += 1
+        events[ev] = val
+        ins.then_inc(T.sem[ev], val)
+        return ev
+
+    for k in range(3):
+        events["arr%d" % k] = len(near_eng) if k == 1 else len(far_eng)
+    events["arrD"] = len(far_eng) + len(near_eng)
+
+    e_hd = mark(S.dma_start(T.hd[:], T.heads[:]), 16)
+    e_pv = mark(S.dma_start(T.pv[:], T.prev[:]), 16)
+    e_d1 = [mark(Q.dma_start(T.d1[:, a:b], T.dur[:, n + a:n + b]), 16) for a, b in T_CHUNKS]
+    e_sh = mark(Q.dma_start(T.sh[:], T.ship[:]), 16)
+    e_d0 = mark(Q.dma_start(T.d0[:], T.dur[:, 0:n]), 16)
+
+    e_w0 = mark(V.memset(T.W[:, 0:FILL], 0.0))
+    e_A = mark(V.memset(T.A[:], BIG))
+    e_k0 = mark(V.memset(T.K[:, 0:16], OFF_T))
+    e_w2 = mark(V.memset(T.W[:, 2 * FILL:n], 0.0))
+    wait("S", e_w0)
+    e_w1 = mark(S.activation(T.W[:, FILL:2 * FILL], T.W[:, 0:FILL], ACT.Silu))
+    e_wg = []
+    for lo, hi in ((n, n + CAP * rank), (n + CAP * (rank + 1), WW)):
+        if hi > lo:
+            e_wg.append(mark(g.iota(T.W[:, lo:hi], [[0, hi - lo]], 0, 0, allow_small_or_imprecise_dtypes=True)))
+    e_dump = mark(g.iota(T.dump[:], [[0, NR], [16, CAP // 16]], n, 1))
+
+    wait("V", e_hd)
+    e_h1 = mark(V.tensor_copy(T.hoff[:, 2:3], T.hd[:, 1:2]))
+    wait("V", e_pv)
+    e_po = mark(V.tensor_copy(T.poff[:], T.pv[:]))
+    wait("V", e_h1, e_A, e_k0)
+    e_m1 = mark(V.tensor_copy(T.A[:, 0:n].indirect(T.hoff[:, 2:3]), T.K[:, 0:16]))
+    e_t = []
+    e_sc = [e_w1]
+    for k, (a, b) in enumerate(T_CHUNKS):
+        wait("V", e_m1, e_d1[k], *e_t)
+        init = OFF_T if k == 0 else T.T1[:, b:b + 1]
+        e_t.append(mark(V.tensor_tensor_scan(T.T1[:, rev(a, b)], T.A[:, rev(a + 1, b + 1)], T.d1[:, rev(a, b)],
+                                             init, ALU.min, ALU.add)))
+        wait("S", e_po, e_w2, *e_wg)
+        wait("S", e_t[k], *e_sc)
+        e_sc.append(mark(S.activation(T.W[:, 0:WW].indirect(T.poff[:, a // 16:b // 16]), T.T1[:, a:b], ACT.Silu)))
+
+    def slot(k):
+        return T.W[:, n + CAP * pr[k]:n + CAP * (pr[k] + 1)]
+
+    def place(k):
+        return T.land[:, CAP * k:CAP * (k + 1)]
+
+    def dst(k):
+        rid, pid = topo.addr(peers[k], core)
+        return DstId(rid=rid, pnc=pid)
+
+    wait("G", e_sc[-1])
+    rid0, pid0 = topo.addr(peers[0], core)
+    g.remote_dma(place(0), slot(0), T.sem.arr0, T.sem.sent, pid0, rid0, bits(far_eng))
+    g.remote_dma_fused([
+        RemoteDMATransfer(dst_ids=[dst(2)], dma_engine_mask=bits(far_eng), remote_sem=T.sem.arr2, src=slot(2), dst=place(2)),
+        RemoteDMATransfer(dst_ids=[dst(1)], dma_engine_mask=bits(near_eng), remote_sem=T.sem.arr1, src=slot(1), dst=place(1)),
+    ], local_sem=T.sem.sent)
+
+    e_k1 = mark(V.memset(T.K[:, 16:32], BIG))
+    e_k2 = mark(V.memset(T.K[:, 32:48], OFF_C))
+    e_h0 = mark(V.tensor_copy(T.hoff[:, 0:1], T.hd[:, 0:1]))
+    wait("V", e_t[-1], e_k1)
+    e_m2 = mark(V.tensor_copy(T.A[:, 0:n].indirect(T.hoff[:, 2:3]), T.K[:, 16:32]))
+    wait("V", e_sh)
+    e_s1 = mark(V.tensor_scalar(T.s1[:], T.sh[:], 4095, None, ALU.bitwise_and))
+    e_go = mark(V.tensor_copy(T.goff[:], T.sh[:]))
+    wait("V", e_m2, e_k2, e_h0)
+    e_m0 = mark(V.tensor_copy(T.A[:, 0:n].indirect(T.hoff[:, 0:1]), T.K[:, 32:48]))
+    wait("V", e_s1, e_dump)
+    e_s2 = mark(V.tensor_tensor(T.s2[:], T.s1[:], T.dump[:], ALU.min))
+    wait("V", e_m0, e_d0)
+    e_c0 = mark(V.tensor_tensor_scan(T.C0[:], T.A[:, 0:n], T.d0[:], OFF_C, ALU.min, ALU.add))
+    e_z0 = mark(V.memset(T.a[:, 0:1], 0.0))
+    e_z1 = mark(V.memset(T.a[:, 961:962], 0.0))
+    e_z2 = mark(V.memset(T.land[:, 960:964], 0.0))
+    wait("V", e_s2)
+    e_so = mark(V.tensor_copy(T.soff[:], T.s2[:]))
+    wait("V", e_c0, e_go)
+    e_a = []
+    for k in range(3):
+        e_a.append(mark(V.tensor_copy(T.a[:, 1 + CAP * k:1 + CAP * (k + 1)],
+                                      T.C0[:, 0:n].indirect(T.goff[:, 20 * pr[k]:20 * (pr[k] + 1)]))))
+    wait("V", e_z0, e_z1, *e_a)
+    e_dl = mark(V.tensor_tensor(T.dl[:, 0:961], T.a[:, 0:961], T.a[:, 1:962], ALU.subtract))
+
+    e_l = []
+    for a, b in BANKS:
+        wait("S", e_c0)
+        e_cp = mark(S.activation(T.Cp[:, a:b], T.C0[:, a:b], ACT.Copy))
+        wait("V", e_cp, e_sc[-1])
+        e_l.append(mark(V.tensor_tensor(T.L[:, a:b], T.W[:, a:b], T.Cp[:, a:b], ALU.add)))
+    wait("V", *e_l)
+    e_last = mark(V.tensor_reduce(T.Dl[:, 0:1], T.L[:, 0:n], AxisListType.X, ALU.max))
+
+    e_run = e_last
+    for k in range(3):
+        lo, hi = CAP * k, CAP * (k + 1) + (1 if k == 2 else 0)
+        wait("V", "arr%d" % k, e_run, e_dl, e_z2)
+        init = T.Dl[:, 0:1] if k == 0 else T.run[:, lo - 1:lo]
+        e_run = mark(V.tensor_tensor_scan(T.run[:, lo:hi], T.dl[:, lo:hi], T.land[:, lo:hi], init, ALU.add, ALU.max))
+        wait("V", e_so, e_last)
+        e_last = mark(V.tensor_tensor(T.L[:, 0:LW].indirect(T.soff[:, 20 * pr[k]:20 * (pr[k] + 1)]),
+                                      place(k), T.a[:, 1 + CAP * k:1 + CAP * (k + 1)], ALU.add))
+
+    wait("G", e_run)
+    mine = T.run[:, 960:961]
+    masks = [bits(far_eng[:half]), bits(near_eng), bits(far_eng[half:])]
+    g.remote_dma_fused([
+        RemoteDMATransfer(dst_ids=[dst(k)], dma_engine_mask=masks[k], remote_sem=T.sem.arrD, src=mine, dst=T.Dland[:, k:k + 1])
+        for k in range(3)], local_sem=T.sem.sent)
+
+    wait("V", e_last)
+    e_m = mark(V.tensor_tensor_scan(T.M[:, rev(0, n)], T.A[:, rev(1, n + 1)], T.L[:, rev(0, n)], OFF_C, ALU.min, ALU.max))
+    wait("V", "arrD", e_run)
+    e_D = mark(V.tensor_tensor_scan(T.Dt[:, 0:3], T.Dland[:, 0:3], T.Dland[:, 0:3], mine, ALU.max, ALU.max))
+    D = T.Dt[:, 2:3]
+    wait("V", e_D, e_m)
+    e_y0 = mark(V.tensor_scalar(T.Y[:, 0:Y_V1], T.M[:, 0:Y_V1], -1.0, D, ALU.mult, ALU.add))
+    e_y2 = mark(V.tensor_scalar(T.Y[:, Y_S:n], T.M[:, Y_S:n], -1.0, D, ALU.mult, ALU.add))
+    wait("S", e_D, e_m)
+    e_y1 = mark(S.activation(T.Y[:, Y_V1:Y_S], T.M[:, Y_V1:Y_S], ACT.Identity, bias=D, scale=-1.0))
+    wait("Q", e_y0)
+    mark(Q.dma_start(T.y[:, 0:Y_V1], T.Y[:, 0:Y_V1]), 16)
+    wait("S", e_y1)
+    mark(S.dma_start(T.y[:, Y_V1:Y_S], T.Y[:, Y_V1:Y_S]), 16)
+    wait("Q", e_y2)
+    mark(Q.dma_start(T.y[:, Y_S:n], T.Y[:, Y_S:n]), 16)
+
+    g.wait_ge(T.sem.sent, 3 * len(far_eng) + 2 * len(near_eng))
+    waited = set()
+    for q in seen:
+        waited |= seen[q]
+    for ev in events:
+        if ev not in waited:
+            wait("G", ev)

@@ -1,47 +1,51 @@
 from concourse.bass import DstId, RemoteDMATransfer
-from concourse.mybir import AluOpType, AxisListType, ActivationFunctionType
+from concourse.mybir import AluOpType, ActivationFunctionType
 
 n, CAP, NR = 1792, 320, 4
+LC = CAP // 16
+DUMP = 432
 WW = n + NR * CAP
-LW = 2240
-OFF_T, OFF_C, BIG = 32.0, 8388608.0, 12582912.0
-T_CHUNKS = [(1536, 1792), (896, 1536), (0, 896)]
-BANKS = [(0, 512), (512, 1024), (1024, 1536), (1536, 1792)]
-FILL = 384
-Y_V1, Y_S = 448, 1120
+OFF, BIG = 32.0, 262144
+T_CHUNKS = [(1600, 1792), (1088, 1600), (0, 1088)]
+S_FILL = 816
+V_CP = 1024
+TAIL = [("scan", 896, 1792, None), ("D", 0, 0, None), ("S", 1344, 1792, "Q"), ("scan", 0, 896, None),
+        ("S", 896, 1344, "Q"), ("V", 0, 448, "Q"), ("S", 448, 896, "S")]
 
 SCRATCH = {
     "d1": ("sbuf", [128, n], "bfloat16"),
     "d0": ("sbuf", [128, n], "bfloat16"),
     "A": ("sbuf", [128, n + 16], "bfloat16"),
-    "K": ("sbuf", [128, 48], "bfloat16"),
+    "K": ("sbuf", [128, 32], "bfloat16"),
     "hd": ("sbuf", [128, 2], "int32"),
+    "sh": ("sbuf", [128, 3 * LC], "int32"),
     "pv": ("sbuf", [128, 112], "int32"),
-    "sh": ("sbuf", [128, 80], "int32"),
     "hoff": ("sbuf", [128, 4], "uint16"),
     "poff": ("sbuf", [128, 112], "uint16"),
-    "goff": ("sbuf", [128, 80], "uint16"),
-    "soff": ("sbuf", [128, 80], "uint16"),
-    "dump": ("sbuf", [128, 80], "int32"),
-    "s1": ("sbuf", [128, 80], "int32"),
-    "s2": ("sbuf", [128, 80], "int32"),
+    "goff": ("sbuf", [128, 3 * LC], "uint16"),
+    "soff": ("sbuf", [128, 3 * LC], "uint16"),
+    "E": ("sbuf", [128, 3 * LC], "int32"),
+    "s1": ("sbuf", [128, 3 * LC], "int32"),
+    "s2": ("sbuf", [128, 3 * LC], "int32"),
     "T1": ("sbuf", [128, n], "float32"),
     "W": ("sbuf", [128, WW], "float32"),
-    "C0": ("sbuf", [128, n], "float32"),
     "Cp": ("psum", [128, 2048], "float32"),
-    "a": ("sbuf", [128, 968], "float32"),
-    "dl": ("sbuf", [128, 968], "float32"),
-    "land": ("sbuf", [128, 968], "float32"),
-    "run": ("sbuf", [128, 968], "float32"),
-    "L": ("sbuf", [128, LW], "float32"),
-    "Dl": ("sbuf", [128, 4], "float32"),
+    "ap": ("psum", [128, 1024], "float32"),
+    "C0": ("sbuf", [128, n], "float32"),
+    "L": ("sbuf", [128, DUMP + n], "float32"),
+    "land": ("sbuf", [128, 3 * CAP + 4], "float32"),
+    "La": ("sbuf", [128, 2 * CAP], "float32"),
+    "a": ("sbuf", [128, CAP + 8], "float32"),
+    "a0": ("sbuf", [128, 2 * CAP], "float32"),
+    "dl": ("sbuf", [128, CAP + 8], "float32"),
+    "run": ("sbuf", [128, n // 2 + 2 * CAP + 8], "float32"),
     "Dland": ("sbuf", [128, 4], "float32"),
     "Dt": ("sbuf", [128, 4], "float32"),
     "M": ("sbuf", [128, n], "float32"),
     "Y": ("sbuf", [128, n], "float32"),
 }
-NEV = 100
-SEMAPHORES = ["e%d" % k for k in range(NEV)] + ["arr0", "arr1", "arr2", "arrD", "sent"]
+NEV = 90
+SEMAPHORES = ["e%d" % k for k in range(NEV)] + ["arr0", "arr1", "arr2", "arrD", "sent", "ship"]
 
 
 def bits(engines):
@@ -90,134 +94,160 @@ def rank_program(g, core, T, topo):
         ins.then_inc(T.sem[ev], val)
         return ev
 
-    for k in range(3):
-        events["arr%d" % k] = len(near_eng) if k == 1 else len(far_eng)
-    events["arrD"] = len(far_eng) + len(near_eng)
+    def fill(buf, a, b, value):
+        return mark(g.iota(buf[:, a:b], [[0, b - a]], value, 0, allow_small_or_imprecise_dtypes=True))
+
+    def part(buf, k, width=CAP):
+        return buf[:, width * k:width * (k + 1)]
+
+    sent = [0]
+
+    def write(transfers):
+        made = []
+        for k, engines, sem, src, dst in transfers:
+            rid, pid = topo.addr(peers[k], core)
+            made.append(RemoteDMATransfer(dst_ids=[DstId(rid=rid, pnc=pid)], dma_engine_mask=bits(engines),
+                                          remote_sem=T.sem[sem], src=src, dst=dst))
+            sent[0] += len(engines)
+        g.remote_dma_fused(made, local_sem=T.sem.sent)
+
+    events.update(arr0=len(far_eng), arr1=len(near_eng), arr2=len(far_eng), arrD=len(far_eng) + len(near_eng), ship=3 * 16)
 
     e_hd = mark(S.dma_start(T.hd[:], T.heads[:]), 16)
     e_pv = mark(S.dma_start(T.pv[:], T.prev[:]), 16)
     e_d1 = [mark(Q.dma_start(T.d1[:, a:b], T.dur[:, n + a:n + b]), 16) for a, b in T_CHUNKS]
-    e_sh = mark(Q.dma_start(T.sh[:], T.ship[:]), 16)
     e_d0 = mark(Q.dma_start(T.d0[:], T.dur[:, 0:n]), 16)
+    for k in range(3):
+        Q.dma_start(part(T.sh, k, LC), part(T.ship, pr[k], LC)).then_inc(T.sem.ship, 16)
 
-    e_w0 = mark(V.memset(T.W[:, 0:FILL], 0.0))
-    e_A = mark(V.memset(T.A[:], BIG))
-    e_k0 = mark(V.memset(T.K[:, 0:16], OFF_T))
-    e_w2 = mark(V.memset(T.W[:, 2 * FILL:n], 0.0))
+    off, big = T.K[:, 0:16], T.K[:, 16:32]
+    e_k0 = mark(V.memset(off, OFF))
+    e_w0 = mark(V.memset(T.W[:, 0:S_FILL], 0.0))
+    e_A = mark(V.memset(T.A[:], float(BIG)))
+    wait("S", e_k0)
+    e_w = [mark(S.activation(T.W[:, n - 16:n], off, ACT.Silu, scale=0.0))]
     wait("S", e_w0)
-    e_w1 = mark(S.activation(T.W[:, FILL:2 * FILL], T.W[:, 0:FILL], ACT.Silu))
-    e_wg = []
-    for lo, hi in ((n, n + CAP * rank), (n + CAP * (rank + 1), WW)):
-        if hi > lo:
-            e_wg.append(mark(g.iota(T.W[:, lo:hi], [[0, hi - lo]], 0, 0, allow_small_or_imprecise_dtypes=True)))
-    e_dump = mark(g.iota(T.dump[:], [[0, NR], [16, CAP // 16]], n, 1))
+    e_w.append(mark(S.activation(T.W[:, S_FILL:2 * S_FILL], T.W[:, 0:S_FILL], ACT.Copy)))
+    e_w += [fill(T.W, lo, hi, 0) for lo, hi in ((n, n + CAP * rank), (n + CAP * (rank + 1), WW)) if hi > lo]
+    e_k1 = fill(T.K, 16, 32, BIG)
+    e_E = mark(g.iota(T.E[:], [[0, 3], [-16, LC]], DUMP, -1))
+    e_z = [fill(T.a, 0, 1, 0), fill(T.a, CAP + 1, CAP + 2, 0), fill(T.land, 3 * CAP, 3 * CAP + 4, 0)]
 
+    def cut(head, value):
+        return mark(V.tensor_copy(T.A[:, 0:n].indirect(head), value))
+
+    head0, head1 = T.hoff[:, 0:1], T.hoff[:, 2:3]
     wait("V", e_hd)
-    e_h1 = mark(V.tensor_copy(T.hoff[:, 2:3], T.hd[:, 1:2]))
+    e_h = mark(V.tensor_copy(T.hoff[:, 0:3:2], T.hd[:]))
+    e_w.append(mark(V.memset(T.W[:, 2 * S_FILL:n - 16], 0.0)))
+    wait("V", e_h, e_A, e_k0)
+    e_t = [cut(head1, off)]
     wait("V", e_pv)
     e_po = mark(V.tensor_copy(T.poff[:], T.pv[:]))
-    wait("V", e_h1, e_A, e_k0)
-    e_m1 = mark(V.tensor_copy(T.A[:, 0:n].indirect(T.hoff[:, 2:3]), T.K[:, 0:16]))
-    e_t = []
-    e_sc = [e_w1]
+    e_sc = []
     for k, (a, b) in enumerate(T_CHUNKS):
-        wait("V", e_m1, e_d1[k], *e_t)
-        init = OFF_T if k == 0 else T.T1[:, b:b + 1]
+        wait("V", e_d1[k], e_t[-1])
+        init = OFF if k == 0 else T.T1[:, b:b + 1]
         e_t.append(mark(V.tensor_tensor_scan(T.T1[:, rev(a, b)], T.A[:, rev(a + 1, b + 1)], T.d1[:, rev(a, b)],
                                              init, ALU.min, ALU.add)))
-        wait("S", e_po, e_w2, *e_wg)
-        wait("S", e_t[k], *e_sc)
+        wait("S", e_po, *e_w)
+        wait("S", e_t[-1], *e_sc)
         e_sc.append(mark(S.activation(T.W[:, 0:WW].indirect(T.poff[:, a // 16:b // 16]), T.T1[:, a:b], ACT.Silu)))
 
-    def slot(k):
-        return T.W[:, n + CAP * pr[k]:n + CAP * (pr[k] + 1)]
-
-    def place(k):
-        return T.land[:, CAP * k:CAP * (k + 1)]
-
-    def dst(k):
-        rid, pid = topo.addr(peers[k], core)
-        return DstId(rid=rid, pnc=pid)
+    def back(k):
+        return k, near_eng if k == 1 else far_eng, "arr%d" % k, T.W[:, n + CAP * pr[k]:n + CAP * (pr[k] + 1)], part(T.land, k)
 
     wait("G", e_sc[-1])
-    rid0, pid0 = topo.addr(peers[0], core)
-    g.remote_dma(place(0), slot(0), T.sem.arr0, T.sem.sent, pid0, rid0, bits(far_eng))
-    g.remote_dma_fused([
-        RemoteDMATransfer(dst_ids=[dst(2)], dma_engine_mask=bits(far_eng), remote_sem=T.sem.arr2, src=slot(2), dst=place(2)),
-        RemoteDMATransfer(dst_ids=[dst(1)], dma_engine_mask=bits(near_eng), remote_sem=T.sem.arr1, src=slot(1), dst=place(1)),
-    ], local_sem=T.sem.sent)
+    write([back(0)])
+    write([back(2), back(1)])
 
-    e_k1 = mark(V.memset(T.K[:, 16:32], BIG))
-    e_k2 = mark(V.memset(T.K[:, 32:48], OFF_C))
-    e_h0 = mark(V.tensor_copy(T.hoff[:, 0:1], T.hd[:, 0:1]))
+    wait("V", "ship", e_E)
+    e_s = mark(V.tensor_tensor(T.s1[:], T.sh[:], T.E[:], ALU.mult))
     wait("V", e_t[-1], e_k1)
-    e_m2 = mark(V.tensor_copy(T.A[:, 0:n].indirect(T.hoff[:, 2:3]), T.K[:, 16:32]))
-    wait("V", e_sh)
-    e_s1 = mark(V.tensor_scalar(T.s1[:], T.sh[:], 4095, None, ALU.bitwise_and))
+    e_m = cut(head1, big)
     e_go = mark(V.tensor_copy(T.goff[:], T.sh[:]))
-    wait("V", e_m2, e_k2, e_h0)
-    e_m0 = mark(V.tensor_copy(T.A[:, 0:n].indirect(T.hoff[:, 0:1]), T.K[:, 32:48]))
-    wait("V", e_s1, e_dump)
-    e_s2 = mark(V.tensor_tensor(T.s2[:], T.s1[:], T.dump[:], ALU.min))
-    wait("V", e_m0, e_d0)
-    e_c0 = mark(V.tensor_tensor_scan(T.C0[:], T.A[:, 0:n], T.d0[:], OFF_C, ALU.min, ALU.add))
-    e_z0 = mark(V.memset(T.a[:, 0:1], 0.0))
-    e_z1 = mark(V.memset(T.a[:, 961:962], 0.0))
-    e_z2 = mark(V.memset(T.land[:, 960:964], 0.0))
-    wait("V", e_s2)
-    e_so = mark(V.tensor_copy(T.soff[:], T.s2[:]))
+    wait("V", e_m)
+    e_m = cut(head0, off)
+    wait("V", e_s)
+    e_s = mark(V.tensor_tensor(T.s2[:], T.s1[:], T.sh[:], ALU.min))
+    wait("V", e_m, e_d0)
+    e_c0 = mark(V.tensor_tensor_scan(T.C0[:], T.A[:, 0:n], T.d0[:], OFF, ALU.min, ALU.add))
+    wait("V", e_s)
+    e_so = mark(V.tensor_scalar(T.soff[:], T.s2[:], DUMP, None, ALU.add))
+
+    def shipped(k):
+        return T.C0[:, 0:n].indirect(part(T.goff, k, LC))
+
+    def target(k):
+        return T.L[:, 0:DUMP + n].indirect(part(T.soff, k, LC))
+
     wait("V", e_c0, e_go)
-    e_a = []
-    for k in range(3):
-        e_a.append(mark(V.tensor_copy(T.a[:, 1 + CAP * k:1 + CAP * (k + 1)],
-                                      T.C0[:, 0:n].indirect(T.goff[:, 20 * pr[k]:20 * (pr[k] + 1)]))))
-    wait("V", e_z0, e_z1, *e_a)
-    e_dl = mark(V.tensor_tensor(T.dl[:, 0:961], T.a[:, 0:961], T.a[:, 1:962], ALU.subtract))
+    e_a = mark(V.tensor_copy(T.a[:, 1:CAP + 1], shipped(2)))
+    e_c = [mark(V.tensor_copy(T.Cp[:, 0:V_CP], T.C0[:, 0:V_CP]))]
+    wait("V", e_a, *e_z)
+    e_dl = mark(V.tensor_tensor(T.dl[:, 0:CAP + 1], T.a[:, 0:CAP + 1], T.a[:, 1:CAP + 2], ALU.subtract))
 
+    wait("S", e_c0, e_go)
+    blocks = [(0, V_CP)]
+    if V_CP < n:
+        blocks.append((V_CP, n))
+        e_c.append(mark(S.activation(T.Cp[:, V_CP:n], T.C0[:, V_CP:n], ACT.Copy)))
+    wait("S", mark(S.activation(T.a0[:], T.C0[:, 0:n].indirect(T.goff[:, 0:2 * LC]), ACT.Copy)))
+    e_ap = [mark(S.activation(T.ap[:, 512 * k:512 * k + CAP], part(T.a0, k), ACT.Copy)) for k in range(2)]
     e_l = []
-    for a, b in BANKS:
-        wait("S", e_c0)
-        e_cp = mark(S.activation(T.Cp[:, a:b], T.C0[:, a:b], ACT.Copy))
-        wait("V", e_cp, e_sc[-1])
-        e_l.append(mark(V.tensor_tensor(T.L[:, a:b], T.W[:, a:b], T.Cp[:, a:b], ALU.add)))
-    wait("V", *e_l)
-    e_last = mark(V.tensor_reduce(T.Dl[:, 0:1], T.L[:, 0:n], AxisListType.X, ALU.max))
+    for e, (a, b) in zip(e_c, blocks):
+        wait("V", e, e_sc[-1])
+        e_l.append(mark(V.tensor_tensor(T.L[:, DUMP + a:DUMP + b], T.W[:, a:b], T.Cp[:, a:b], ALU.add)))
 
-    e_run = e_last
-    for k in range(3):
-        lo, hi = CAP * k, CAP * (k + 1) + (1 if k == 2 else 0)
-        wait("V", "arr%d" % k, e_run, e_dl, e_z2)
-        init = T.Dl[:, 0:1] if k == 0 else T.run[:, lo - 1:lo]
-        e_run = mark(V.tensor_tensor_scan(T.run[:, lo:hi], T.dl[:, lo:hi], T.land[:, lo:hi], init, ALU.add, ALU.max))
-        wait("V", e_so, e_last)
-        e_last = mark(V.tensor_tensor(T.L[:, 0:LW].indirect(T.soff[:, 20 * pr[k]:20 * (pr[k] + 1)]),
-                                      place(k), T.a[:, 1 + CAP * k:1 + CAP * (k + 1)], ALU.add))
+    done = [0]
+
+    def carry(width, in0, in1, op0):
+        lo = done[0]
+        done[0] += width
+        init = 0.0 if lo == 0 else T.run[:, lo - 1:lo]
+        return mark(V.tensor_tensor_scan(T.run[:, lo:lo + width], in0, in1, init, op0, ALU.max))
+
+    wait("V", *e_l)
+    e_run = carry(n // 2, T.L[:, DUMP:DUMP + n // 2], T.L[:, DUMP + n // 2:DUMP + n], ALU.max)
+    e_l.append(e_run)
+
+    for k in range(2):
+        wait("V", "arr%d" % k, e_ap[k])
+        e_la = mark(V.tensor_tensor(part(T.La, k), part(T.land, k), T.ap[:, 512 * k:512 * k + CAP], ALU.add))
+        wait("S", e_la, e_so, *e_l)
+        e_l.append(mark(S.activation(target(k), part(T.La, k), ACT.Silu)))
+        wait("V", e_run, e_la)
+        e_run = carry(CAP // 2, part(T.La, 2 * k, CAP // 2), part(T.La, 2 * k + 1, CAP // 2), ALU.max)
+
+    wait("V", "arr2", e_run, e_dl)
+    e_run = carry(CAP + 1, T.dl[:, 0:CAP + 1], T.land[:, 2 * CAP:3 * CAP + 1], ALU.add)
+    wait("V", e_so, e_l[-1])
+    e_l.append(mark(V.tensor_tensor(target(2), part(T.land, 2), T.a[:, 1:CAP + 1], ALU.add)))
 
     wait("G", e_run)
-    mine = T.run[:, 960:961]
-    masks = [bits(far_eng[:half]), bits(near_eng), bits(far_eng[half:])]
-    g.remote_dma_fused([
-        RemoteDMATransfer(dst_ids=[dst(k)], dma_engine_mask=masks[k], remote_sem=T.sem.arrD, src=mine, dst=T.Dland[:, k:k + 1])
-        for k in range(3)], local_sem=T.sem.sent)
+    mine = T.run[:, done[0] - 1:done[0]]
+    split = [far_eng[:half], near_eng, far_eng[half:]]
+    write([(k, split[k], "arrD", mine, T.Dland[:, k:k + 1]) for k in range(3)])
 
-    wait("V", e_last)
-    e_m = mark(V.tensor_tensor_scan(T.M[:, rev(0, n)], T.A[:, rev(1, n + 1)], T.L[:, rev(0, n)], OFF_C, ALU.min, ALU.max))
-    wait("V", "arrD", e_run)
-    e_D = mark(V.tensor_tensor_scan(T.Dt[:, 0:3], T.Dland[:, 0:3], T.Dland[:, 0:3], mine, ALU.max, ALU.max))
     D = T.Dt[:, 2:3]
-    wait("V", e_D, e_m)
-    e_y0 = mark(V.tensor_scalar(T.Y[:, 0:Y_V1], T.M[:, 0:Y_V1], -1.0, D, ALU.mult, ALU.add))
-    e_y2 = mark(V.tensor_scalar(T.Y[:, Y_S:n], T.M[:, Y_S:n], -1.0, D, ALU.mult, ALU.add))
-    wait("S", e_D, e_m)
-    e_y1 = mark(S.activation(T.Y[:, Y_V1:Y_S], T.M[:, Y_V1:Y_S], ACT.Identity, bias=D, scale=-1.0))
-    wait("Q", e_y0)
-    mark(Q.dma_start(T.y[:, 0:Y_V1], T.Y[:, 0:Y_V1]), 16)
-    wait("S", e_y1)
-    mark(S.dma_start(T.y[:, Y_V1:Y_S], T.Y[:, Y_V1:Y_S]), 16)
-    wait("Q", e_y2)
-    mark(Q.dma_start(T.y[:, Y_S:n], T.Y[:, Y_S:n]), 16)
+    e_m, e_D = [(n, e_l[-1])], None
+    for step, a, b, store in TAIL:
+        if step == "scan":
+            wait("V", e_m[-1][1])
+            init = 0.0 if b == n else T.M[:, b:b + 1]
+            e_m.append((a, mark(V.tensor_tensor_scan(T.M[:, rev(a, b)], T.A[:, rev(a + 1, b + 1)],
+                                                     T.L[:, rev(DUMP + a, DUMP + b)], init, ALU.min, ALU.max))))
+        elif step == "D":
+            wait("V", "arrD", e_run)
+            e_D = mark(V.tensor_tensor_scan(T.Dt[:, 0:3], T.Dland[:, 0:3], T.Dland[:, 0:3], mine, ALU.max, ALU.max))
+        else:
+            wait(step, e_D, [e for lo, e in e_m if lo <= a][0])
+            e_y = mark(S.activation(T.Y[:, a:b], T.M[:, a:b], ACT.Identity, bias=D, scale=-1.0) if step == "S" else
+                       V.tensor_scalar(T.Y[:, a:b], T.M[:, a:b], -1.0, D, ALU.mult, ALU.add))
+            wait(store, e_y)
+            mark(queues[store].dma_start(T.y[:, a:b], T.Y[:, a:b]), 16)
 
-    g.wait_ge(T.sem.sent, 3 * len(far_eng) + 2 * len(near_eng))
+    g.wait_ge(T.sem.sent, sent[0])
     waited = set()
     for q in seen:
         waited |= seen[q]

from concourse.bass import DstId, RemoteDMATransfer
from concourse.mybir import AluOpType, ActivationFunctionType

n, CAP, NR = 1792, 320, 4
LC = CAP // 16
DUMP = 432
WW = n + NR * CAP
OFF, BIG = 32.0, 262144
T_CHUNKS = [(1600, 1792), (1088, 1600), (0, 1088)]
S_FILL = 816
V_CP = 1024
TAIL = [("scan", 896, 1792, None), ("D", 0, 0, None), ("S", 1344, 1792, "Q"), ("scan", 0, 896, None),
        ("S", 896, 1344, "Q"), ("V", 0, 448, "Q"), ("S", 448, 896, "S")]

SCRATCH = {
    "d1": ("sbuf", [128, n], "bfloat16"),
    "d0": ("sbuf", [128, n], "bfloat16"),
    "A": ("sbuf", [128, n + 16], "bfloat16"),
    "K": ("sbuf", [128, 32], "bfloat16"),
    "hd": ("sbuf", [128, 2], "int32"),
    "sh": ("sbuf", [128, 3 * LC], "int32"),
    "pv": ("sbuf", [128, 112], "int32"),
    "hoff": ("sbuf", [128, 4], "uint16"),
    "poff": ("sbuf", [128, 112], "uint16"),
    "goff": ("sbuf", [128, 3 * LC], "uint16"),
    "soff": ("sbuf", [128, 3 * LC], "uint16"),
    "E": ("sbuf", [128, 3 * LC], "int32"),
    "s1": ("sbuf", [128, 3 * LC], "int32"),
    "s2": ("sbuf", [128, 3 * LC], "int32"),
    "T1": ("sbuf", [128, n], "float32"),
    "W": ("sbuf", [128, WW], "float32"),
    "Cp": ("psum", [128, 2048], "float32"),
    "ap": ("psum", [128, 1024], "float32"),
    "C0": ("sbuf", [128, n], "float32"),
    "L": ("sbuf", [128, DUMP + n], "float32"),
    "land": ("sbuf", [128, 3 * CAP + 4], "float32"),
    "La": ("sbuf", [128, 2 * CAP], "float32"),
    "a": ("sbuf", [128, CAP + 8], "float32"),
    "a0": ("sbuf", [128, 2 * CAP], "float32"),
    "dl": ("sbuf", [128, CAP + 8], "float32"),
    "run": ("sbuf", [128, n // 2 + 2 * CAP + 8], "float32"),
    "Dland": ("sbuf", [128, 4], "float32"),
    "Dt": ("sbuf", [128, 4], "float32"),
    "M": ("sbuf", [128, n], "float32"),
    "Y": ("sbuf", [128, n], "float32"),
}
NEV = 90
SEMAPHORES = ["e%d" % k for k in range(NEV)] + ["arr0", "arr1", "arr2", "arrD", "sent", "ship"]


def bits(engines):
    m = 0
    for e in engines:
        m |= 1 << e
    return m


def rev(a, b):
    return slice(b - 1, a - 1 if a > 0 else None, -1)


def rank_program(g, core, T, topo):
    rank = T.rank_of(core)
    if rank is None:
        return
    ALU, ACT = AluOpType, ActivationFunctionType
    V, S, Q = g.vector, g.scalar, g.sync
    queues = {"G": g, "V": V, "S": S, "Q": Q}

    others = [c for c in T.cores if c != core]
    near = [c for c in others if c in topo.cores_of(core)]
    far = [c for c in others if c not in near]
    far = [c for c in far if topo.die(c) == topo.die(core)] + [c for c in far if topo.die(c) != topo.die(core)]
    peers = [far[0], near[0], far[1]]
    pr = [T.rank_of(c) for c in peers]
    far_eng = topo.engines(core, far[0])
    near_eng = [e for e in topo.engines(core, near[0]) if e not in far_eng]
    half = len(far_eng) // 2

    count = [0]
    seen = {q: set() for q in queues}
    events = {}

    def wait(q, *evs):
        for ev in evs:
            if ev not in seen[q]:
                seen[q].add(ev)
                queues[q].wait_ge(T.sem[ev], events[ev])

    def mark(ins, val=1):
        ev = "e%d" % count[0]
        count[0] += 1
        events[ev] = val
        ins.then_inc(T.sem[ev], val)
        return ev

    def fill(buf, a, b, value):
        return mark(g.iota(buf[:, a:b], [[0, b - a]], value, 0, allow_small_or_imprecise_dtypes=True))

    def part(buf, k, width=CAP):
        return buf[:, width * k:width * (k + 1)]

    sent = [0]

    def write(transfers):
        made = []
        for k, engines, sem, src, dst in transfers:
            rid, pid = topo.addr(peers[k], core)
            made.append(RemoteDMATransfer(dst_ids=[DstId(rid=rid, pnc=pid)], dma_engine_mask=bits(engines),
                                          remote_sem=T.sem[sem], src=src, dst=dst))
            sent[0] += len(engines)
        g.remote_dma_fused(made, local_sem=T.sem.sent)

    events.update(arr0=len(far_eng), arr1=len(near_eng), arr2=len(far_eng), arrD=len(far_eng) + len(near_eng), ship=3 * 16)

    e_hd = mark(S.dma_start(T.hd[:], T.heads[:]), 16)
    e_pv = mark(S.dma_start(T.pv[:], T.prev[:]), 16)
    e_d1 = [mark(Q.dma_start(T.d1[:, a:b], T.dur[:, n + a:n + b]), 16) for a, b in T_CHUNKS]
    e_d0 = mark(Q.dma_start(T.d0[:], T.dur[:, 0:n]), 16)
    for k in range(3):
        Q.dma_start(part(T.sh, k, LC), part(T.ship, pr[k], LC)).then_inc(T.sem.ship, 16)

    off, big = T.K[:, 0:16], T.K[:, 16:32]
    e_k0 = mark(V.memset(off, OFF))
    e_w0 = mark(V.memset(T.W[:, 0:S_FILL], 0.0))
    e_A = mark(V.memset(T.A[:], float(BIG)))
    wait("S", e_k0)
    e_w = [mark(S.activation(T.W[:, n - 16:n], off, ACT.Silu, scale=0.0))]
    wait("S", e_w0)
    e_w.append(mark(S.activation(T.W[:, S_FILL:2 * S_FILL], T.W[:, 0:S_FILL], ACT.Copy)))
    e_w += [fill(T.W, lo, hi, 0) for lo, hi in ((n, n + CAP * rank), (n + CAP * (rank + 1), WW)) if hi > lo]
    e_k1 = fill(T.K, 16, 32, BIG)
    e_E = mark(g.iota(T.E[:], [[0, 3], [-16, LC]], DUMP, -1))
    e_z = [fill(T.a, 0, 1, 0), fill(T.a, CAP + 1, CAP + 2, 0), fill(T.land, 3 * CAP, 3 * CAP + 4, 0)]

    def cut(head, value):
        return mark(V.tensor_copy(T.A[:, 0:n].indirect(head), value))

    head0, head1 = T.hoff[:, 0:1], T.hoff[:, 2:3]
    wait("V", e_hd)
    e_h = mark(V.tensor_copy(T.hoff[:, 0:3:2], T.hd[:]))
    e_w.append(mark(V.memset(T.W[:, 2 * S_FILL:n - 16], 0.0)))
    wait("V", e_h, e_A, e_k0)
    e_t = [cut(head1, off)]
    wait("V", e_pv)
    e_po = mark(V.tensor_copy(T.poff[:], T.pv[:]))
    e_sc = []
    for k, (a, b) in enumerate(T_CHUNKS):
        wait("V", e_d1[k], e_t[-1])
        init = OFF if k == 0 else T.T1[:, b:b + 1]
        e_t.append(mark(V.tensor_tensor_scan(T.T1[:, rev(a, b)], T.A[:, rev(a + 1, b + 1)], T.d1[:, rev(a, b)],
                                             init, ALU.min, ALU.add)))
        wait("S", e_po, *e_w)
        wait("S", e_t[-1], *e_sc)
        e_sc.append(mark(S.activation(T.W[:, 0:WW].indirect(T.poff[:, a // 16:b // 16]), T.T1[:, a:b], ACT.Silu)))

    def back(k):
        return k, near_eng if k == 1 else far_eng, "arr%d" % k, T.W[:, n + CAP * pr[k]:n + CAP * (pr[k] + 1)], part(T.land, k)

    wait("G", e_sc[-1])
    write([back(0)])
    write([back(2), back(1)])

    wait("V", "ship", e_E)
    e_s = mark(V.tensor_tensor(T.s1[:], T.sh[:], T.E[:], ALU.mult))
    wait("V", e_t[-1], e_k1)
    e_m = cut(head1, big)
    e_go = mark(V.tensor_copy(T.goff[:], T.sh[:]))
    wait("V", e_m)
    e_m = cut(head0, off)
    wait("V", e_s)
    e_s = mark(V.tensor_tensor(T.s2[:], T.s1[:], T.sh[:], ALU.min))
    wait("V", e_m, e_d0)
    e_c0 = mark(V.tensor_tensor_scan(T.C0[:], T.A[:, 0:n], T.d0[:], OFF, ALU.min, ALU.add))
    wait("V", e_s)
    e_so = mark(V.tensor_scalar(T.soff[:], T.s2[:], DUMP, None, ALU.add))

    def shipped(k):
        return T.C0[:, 0:n].indirect(part(T.goff, k, LC))

    def target(k):
        return T.L[:, 0:DUMP + n].indirect(part(T.soff, k, LC))

    wait("V", e_c0, e_go)
    e_a = mark(V.tensor_copy(T.a[:, 1:CAP + 1], shipped(2)))
    e_c = [mark(V.tensor_copy(T.Cp[:, 0:V_CP], T.C0[:, 0:V_CP]))]
    wait("V", e_a, *e_z)
    e_dl = mark(V.tensor_tensor(T.dl[:, 0:CAP + 1], T.a[:, 0:CAP + 1], T.a[:, 1:CAP + 2], ALU.subtract))

    wait("S", e_c0, e_go)
    blocks = [(0, V_CP)]
    if V_CP < n:
        blocks.append((V_CP, n))
        e_c.append(mark(S.activation(T.Cp[:, V_CP:n], T.C0[:, V_CP:n], ACT.Copy)))
    wait("S", mark(S.activation(T.a0[:], T.C0[:, 0:n].indirect(T.goff[:, 0:2 * LC]), ACT.Copy)))
    e_ap = [mark(S.activation(T.ap[:, 512 * k:512 * k + CAP], part(T.a0, k), ACT.Copy)) for k in range(2)]
    e_l = []
    for e, (a, b) in zip(e_c, blocks):
        wait("V", e, e_sc[-1])
        e_l.append(mark(V.tensor_tensor(T.L[:, DUMP + a:DUMP + b], T.W[:, a:b], T.Cp[:, a:b], ALU.add)))

    done = [0]

    def carry(width, in0, in1, op0):
        lo = done[0]
        done[0] += width
        init = 0.0 if lo == 0 else T.run[:, lo - 1:lo]
        return mark(V.tensor_tensor_scan(T.run[:, lo:lo + width], in0, in1, init, op0, ALU.max))

    wait("V", *e_l)
    e_run = carry(n // 2, T.L[:, DUMP:DUMP + n // 2], T.L[:, DUMP + n // 2:DUMP + n], ALU.max)
    e_l.append(e_run)

    for k in range(2):
        wait("V", "arr%d" % k, e_ap[k])
        e_la = mark(V.tensor_tensor(part(T.La, k), part(T.land, k), T.ap[:, 512 * k:512 * k + CAP], ALU.add))
        wait("S", e_la, e_so, *e_l)
        e_l.append(mark(S.activation(target(k), part(T.La, k), ACT.Silu)))
        wait("V", e_run, e_la)
        e_run = carry(CAP // 2, part(T.La, 2 * k, CAP // 2), part(T.La, 2 * k + 1, CAP // 2), ALU.max)

    wait("V", "arr2", e_run, e_dl)
    e_run = carry(CAP + 1, T.dl[:, 0:CAP + 1], T.land[:, 2 * CAP:3 * CAP + 1], ALU.add)
    wait("V", e_so, e_l[-1])
    e_l.append(mark(V.tensor_tensor(target(2), part(T.land, 2), T.a[:, 1:CAP + 1], ALU.add)))

    wait("G", e_run)
    mine = T.run[:, done[0] - 1:done[0]]
    split = [far_eng[:half], near_eng, far_eng[half:]]
    write([(k, split[k], "arrD", mine, T.Dland[:, k:k + 1]) for k in range(3)])

    D = T.Dt[:, 2:3]
    e_m, e_D = [(n, e_l[-1])], None
    for step, a, b, store in TAIL:
        if step == "scan":
            wait("V", e_m[-1][1])
            init = 0.0 if b == n else T.M[:, b:b + 1]
            e_m.append((a, mark(V.tensor_tensor_scan(T.M[:, rev(a, b)], T.A[:, rev(a + 1, b + 1)],
                                                     T.L[:, rev(DUMP + a, DUMP + b)], init, ALU.min, ALU.max))))
        elif step == "D":
            wait("V", "arrD", e_run)
            e_D = mark(V.tensor_tensor_scan(T.Dt[:, 0:3], T.Dland[:, 0:3], T.Dland[:, 0:3], mine, ALU.max, ALU.max))
        else:
            wait(step, e_D, [e for lo, e in e_m if lo <= a][0])
            e_y = mark(S.activation(T.Y[:, a:b], T.M[:, a:b], ACT.Identity, bias=D, scale=-1.0) if step == "S" else
                       V.tensor_scalar(T.Y[:, a:b], T.M[:, a:b], -1.0, D, ALU.mult, ALU.add))
            wait(store, e_y)
            mark(queues[store].dma_start(T.y[:, a:b], T.Y[:, a:b]), 16)

    g.wait_ge(T.sem.sent, sent[0])
    waited = set()
    for q in seen:
        waited |= seen[q]
    for ev in events:
        if ev not in waited:
            wait("G", ev)
